import numpy as np
import ml_dtypes


def mxq(x, axis, fmt="e4m3"):
    dtype, down = {"e4m3": (ml_dtypes.float8_e4m3fn, 7), "e5m2": (ml_dtypes.float8_e5m2, 14)}[fmt]
    v = np.moveaxis(np.asarray(x, np.float32).astype(ml_dtypes.bfloat16).astype(np.float64), axis, -1)
    blocks = v.reshape(v.shape[:-1] + (-1, 32))
    amax = np.abs(blocks).max(-1, keepdims=True)
    byte = np.maximum(np.where(amax > 0, np.frexp(amax)[1] - 1 + 127, 0) - down, 1)
    scale = np.exp2(byte - 127.0)
    codes = (blocks / scale).astype(np.float32).astype(dtype).astype(np.float64)
    return np.moveaxis((codes * scale).reshape(v.shape), -1, axis)


WIDE = False


def mx_kscale(k):
    if not WIDE:
        return np.ones(k)
    levels = np.array([10, -10, 5, -5, 0])
    if k % 512:
        return np.exp2(np.random.permutation(np.resize(levels, k // 32))).repeat(32)
    a = np.empty((k // 512, 16))
    for p in range(k // 512):
        a[p, :8] = np.random.permutation(np.resize(levels, 8))
        for g in range(8):
            far = levels[np.abs(levels - a[p, g]) >= 10]
            a[p, g + 8] = far[np.random.randint(len(far))]
    return np.exp2(a.ravel()).repeat(32)


def f64(x):
    return np.asarray(x).astype(np.float64)


def striped(idx):
    return np.tile(np.asarray(idx).reshape(-1, 16).T, (8, 1)).astype(np.uint16)


def unstriped(offs):
    return offs[:16].T.reshape(-1).astype(np.int64)


def striped8(idx):
    return np.asarray(idx).reshape(8, -1, 16).transpose(0, 2, 1).reshape(128, -1).astype(np.uint16)


def unstriped8(offs):
    return offs.reshape(8, 16, -1).transpose(0, 2, 1).reshape(8, -1).astype(np.int64)


def pick8(x, idx, run):
    r = np.arange(len(x))
    return x[r[:, None], idx[r % (8 * run) // run]]


E2M1 = np.array([0.0, 0.5, 1.0, 1.5, 2.0, 3.0, 4.0, 6.0, -0.0, -0.5, -1.0, -1.5, -2.0, -3.0, -4.0, -6.0])


def pack_weight(w, fmt):
    k, n = w.shape
    w = f64(np.asarray(w, np.float32).astype(ml_dtypes.bfloat16)).reshape(k // 32, 32, n)
    amax = np.abs(w).max(1)
    if fmt == "e4m3":
        byte = np.frexp(amax)[1] - 1 + 127 - 7
    else:
        mant, ex = np.frexp(amax / 6.0)
        byte = np.where(mant > 0.5, ex, ex - 1) + 127
    byte = np.clip(np.where(amax > 0, byte, 1), 1, 254)
    scaled = (w * np.exp2(127.0 - byte)[:, None, :]).reshape(k, n).astype(np.float32)
    by_word = np.ascontiguousarray(scaled.reshape(k // 512, 128, 4, n).transpose(0, 1, 3, 2))
    if fmt == "e4m3":
        words = by_word.astype(ml_dtypes.float8_e4m3fn).view(np.uint8)
    else:
        c = by_word.astype(ml_dtypes.float4_e2m1fn).view(np.uint8) & 0xF
        words = (c[..., 0::2] | (c[..., 1::2] << 4)).reshape(k // 512, 128, 2 * n)
    return np.ascontiguousarray(words), np.ascontiguousarray(byte.astype(np.uint8).reshape(k // 512, 16, n))


def unpack_weight(words, scales, fmt):
    g, _, n = scales.shape
    words = np.ascontiguousarray(words).reshape(g, 128, n, -1)
    if fmt == "e4m3":
        vals = words.view(ml_dtypes.float8_e4m3fn).astype(np.float64)
    else:
        nib = np.empty((g, 128, n, 4), np.uint8)
        nib[..., 0::2] = words & 0xF
        nib[..., 1::2] = words >> 4
        vals = E2M1[nib]
    vals = vals * np.repeat(np.exp2(scales.astype(np.float64) - 127.0), 8, axis=1)[..., None]
    return vals.transpose(0, 1, 3, 2).reshape(g * 512, n)


def bf(x):
    return np.asarray(x, np.float32).astype(ml_dtypes.bfloat16)


def planes(Y):
    r, m = Y.shape
    b = f64(bf(Y)).reshape(r // 32, 32, m)
    amax = np.abs(b).max(1)
    byte = np.clip(np.where(amax > 0, np.frexp(amax)[1] - 1 + 127 - 7, 1), 1, 254)
    codes = (b * np.exp2(127.0 - byte)[:, None, :]).reshape(r, m).astype(np.float32).astype(ml_dtypes.float8_e4m3fn).view(np.uint8)
    words = codes.reshape(r // 512, 128, 4, m).transpose(0, 1, 3, 2)
    return np.ascontiguousarray(words), np.ascontiguousarray(byte.astype(np.uint8).reshape(r // 512, 16, m))


K, T, J, L, S, N = 512, 1024, 512, 512, 1024, 512


def setup_inputs():
    n = np.random.standard_normal
    idx = np.stack([np.random.permutation(T)[:J] for _ in range(8)])
    idx2 = np.random.permutation(S)[:J]
    fk = mx_kscale(K)
    fl = mx_kscale(L)
    wap = pack_weight(n((K, N)) * 1 / np.sqrt(K) * fk[:, None], "e2m1")
    xbp = pack_weight(n((L, S)) / fl[:, None], "e4m3")
    wbp = pack_weight(n((L, N)) * 1 / np.sqrt(L) * fl[:, None], "e2m1")
    return {
        "xt": (n((K, T)) / fk[:, None]).astype(np.float32),
        "wa_words": wap[0],
        "wa_scales": wap[1],
        "xb_words": xbp[0],
        "xb_scales": xbp[1],
        "wb_words": wbp[0],
        "wb_scales": wbp[1],
        "offs": striped8(idx),
        "offs2": striped(idx2),
    }


def reference(xt, wa_words, wa_scales, xb_words, xb_scales, wb_words, wb_scales, offs, offs2):
    idx = unstriped8(offs)
    idx2 = unstriped(offs2)
    wau = unpack_weight(wa_words, wa_scales, "e2m1")
    xbu = unpack_weight(xb_words, xb_scales, "e4m3")
    wbu = unpack_weight(wb_words, wb_scales, "e2m1")
    xtidxq = mxq(pick8(f64(xt), idx, 64), 0, "e4m3")
    p = wau.T @ xtidxq
    xbidx2g = xbu[:, idx2]
    q = wbu.T @ xbidx2g
    y = np.maximum(p - 0.7 * q, 0.0)
    words, scales = planes(y)
    return y, words, scales

@@ -1,0 +1,202 @@
+from contextlib import ExitStack
+
+import concourse.mybir as mybir
+
+K, T, J, L, S, N = 512, 1024, 512, 512, 1024, 512
+FLOPS = 2 * K * N * J + 2 * L * N * J
+
+F32 = mybir.dt.float32
+BF16 = mybir.dt.bfloat16
+I32 = mybir.dt.int32
+U32 = mybir.dt.uint32
+U16 = mybir.dt.uint16
+U8 = mybir.dt.uint8
+FP8X4 = mybir.dt.float8_e4m3fn_x4
+FP4X4 = mybir.dt.float4_e2m1fn_x4
+ACT = mybir.ActivationFunctionType
+ALU = mybir.AluOpType
+
+P = 128
+PACK = 4
+CH = 128
+GCH = 256
+HALF = T // 2
+
+
+def tile_moe_expert_heads_against_shared_pl_kernel(
+    tc, xt, wa_words, wa_scales, xb_words, xb_scales, wb_words, wb_scales, offs, offs2, out_0, out_1, out_2
+):
+    nc = tc.nc
+    with ExitStack() as ctx:
+        sb = ctx.enter_context(tc.tile_pool(name="sb", bufs=1))
+        ps = ctx.enter_context(tc.psum_pool(name="ps", bufs=1))
+
+        def tile(shape, dtype, name):
+            return sb.tile(shape, dtype, name=name, align_bytes=64)
+
+        lists = sb.tile([P, J // 16], U16, name="lists")
+        list2 = sb.tile([P, J // 16], U16, name="list2")
+        xb_w = tile([P, S], U32, "xb_w")
+        xb_s = tile([P, S], U8, "xb_s")
+        wa_w = tile([P, 2 * N], U8, "wa_w")
+        wb_w = tile([P, 2 * N], U8, "wb_w")
+        wa_s = tile([P, N], U8, "wa_s")
+        wb_s = tile([P, N], U8, "wb_s")
+        raw = [[tile([P, 2, HALF], F32, "raw%d%d" % (u, h)) for h in range(2)] for u in range(2)]
+        pairs = [tile([P, T], F32, "pairs%d" % u) for u in range(2)]
+
+        def load_scales(engine, plane, rows, quads):
+            for q in quads:
+                engine.dma_start(out=plane[32 * q : 32 * q + 4, :].bitcast(I32), in_=rows[0, 4 * q : 4 * q + 4, :].bitcast(I32))
+
+        def load_xt(u, h):
+            rows = xt.rearrange("(p t) c -> p t c", t=PACK)
+            nc.sync.dma_start(out=raw[u][h][:], in_=rows[:, 2 * u : 2 * u + 2, h * HALF : (h + 1) * HALF])
+
+        nc.vector.memset(xb_s[:].bitcast(I32), 0)
+        nc.vector.memset(wb_s[:].bitcast(I32), 0)
+        nc.gpsimd.memset(wa_s[:].bitcast(I32), 0)
+
+        nc.sync.dma_start(list2[:], offs2)
+        nc.sync.dma_start(lists[:], offs)
+        nc.sync.dma_start(out=xb_w[:].bitcast(I32), in_=xb_words[0].rearrange("p c r -> p (c r)").bitcast(I32))
+        load_xt(0, 0)
+        load_scales(nc.sync, xb_s, xb_scales, range(4))
+        load_scales(nc.gpsimd, wa_s, wa_scales, range(4))
+        load_xt(0, 1)
+        nc.sync.dma_start(out=wb_w[:].bitcast(I32), in_=wb_words[0].bitcast(I32))
+        load_xt(1, 0)
+        load_scales(nc.sync, wb_s, wb_scales, range(4))
+        load_xt(1, 1)
+        nc.sync.dma_start(out=wa_w[:].bitcast(I32), in_=wa_words[0].bitcast(I32))
+
+        def cast(engine, u, h, lo, hi):
+            dst = pairs[u][:].bitcast(BF16).rearrange("p (c e) -> p c e", e=2)[:, h * HALF + lo : h * HALF + hi, :]
+            src = raw[u][h][:, :, lo:hi].rearrange("p e c -> p c e")
+            if engine == "scalar":
+                nc.scalar.activation(out=dst, in_=src, func=ACT.Copy)
+            else:
+                nc.vector.tensor_copy(out=dst, in_=src)
+
+        def deal(words, plane, name):
+            dealt_w = tile([P, 2 * N], U8, name + "_w")
+            dealt_s = tile([P, N], U8, name + "_s")
+            nc.vector.tensor_copy(
+                out=dealt_w[:].bitcast(U16).rearrange("p (t b i) -> p b t i", t=PACK, i=8),
+                in_=words[:].bitcast(U16).rearrange("p (b i t) -> p b t i", t=PACK, i=8),
+            )
+            nc.vector.tensor_copy(
+                out=dealt_s[:].rearrange("p (t b i) -> p b t i", t=PACK, i=16),
+                in_=plane[:].rearrange("p (b i t) -> p b t i", t=PACK, i=16),
+            )
+            return dealt_w, dealt_s
+
+        def product(bank, w, codes, scales, lo):
+            for t in range(PACK):
+                nc.tensor.matmul_mx(
+                    out=bank[:, t, :],
+                    lhsT=w[0][:, 2 * P * t : 2 * P * (t + 1)].bitcast(FP4X4),
+                    lhsT_scale=w[1][:, P * t : P * (t + 1)],
+                    rhs=codes[:, lo : lo + CH].bitcast(FP8X4),
+                    rhs_scale=scales[:, lo : lo + CH],
+                    start=True,
+                    stop=True,
+                )
+
+        xbg_w = tile([P, J], U32, "xbg_w")
+        xbg_s = tile([P, J], U8, "xbg_s")
+        nc.vector.tensor_copy(out=xbg_w[:], in_=xb_w[:].indirect(list2[:]))
+        cast("scalar", 0, 0, 0, HALF)
+        nc.vector.tensor_copy(out=xbg_s[:], in_=xb_s[:].indirect(list2[:]))
+        cast("scalar", 0, 1, 0, HALF)
+
+        picked = [tile([P, 2, GCH], F32, "picked%d" % g) for g in range(J // GCH)]
+
+        def gather(u, g):
+            cols = GCH // 16
+            nc.vector.tensor_copy(out=picked[g][:, u, :], in_=pairs[u][:].indirect(lists[:, g * cols : (g + 1) * cols]))
+
+        gather(0, 0)
+        gather(0, 1)
+        cast("scalar", 1, 0, 0, HALF)
+        wb = deal(wb_w, wb_s, "wbd")
+        q_banks = [ps.tile([P, PACK, CH], F32, name="q%d" % c) for c in range(J // CH)]
+        for c in range(J // CH):
+            product(q_banks[c], wb, xbg_w, xbg_s, c * CH)
+        SPLIT = 176
+        cast("scalar", 1, 1, 0, SPLIT)
+        cast("vector", 1, 1, SPLIT, HALF)
+
+        q_off = [tile([P, CH, PACK], F32, "q_off%d" % c) for c in range(J // CH)]
+        for c in range(J // CH):
+            nc.scalar.activation(out=q_off[c][:], in_=q_banks[c][:].rearrange("p t j -> p j t"), func=ACT.Copy, scale=-0.7)
+
+        woven = [tile([P, GCH, 2], F32, "woven%d" % g) for g in range(J // GCH)]
+        x_w = [tile([P, GCH], U32, "x_w%d" % g) for g in range(J // GCH)]
+        x_s = [tile([P, GCH], U8, "x_s%d" % g) for g in range(J // GCH)]
+
+        def weave(g):
+            nc.vector.tensor_copy(out=woven[g][:], in_=picked[g][:].rearrange("p u j -> p j u"))
+
+        def quantise_x(g):
+            nc.vector.quantize_mx(
+                out=x_w[g][:].bitcast(FP8X4), scales=x_s[g][:], in_=woven[g][:].rearrange("p j u -> p (j u)").bitcast(BF16)
+            )
+
+        p_banks = [ps.tile([P, PACK, CH], F32, name="p%d" % c) for c in range(J // CH)]
+
+        def routed(g):
+            for c in range(g * GCH // CH, (g + 1) * GCH // CH):
+                product(p_banks[c], wa, x_w[g], x_s[g], c * CH - g * GCH)
+
+        gather(1, 0)
+        weave(0)
+        wa = deal(wa_w, wa_s, "wad")
+        quantise_x(0)
+        routed(0)
+        gather(1, 1)
+        weave(1)
+        quantise_x(1)
+        routed(1)
+
+        diff = [tile([P, CH, PACK], F32, "diff%d" % c) for c in range(J // CH)]
+        y = [tile([P, PACK, CH], F32, "y%d" % c) for c in range(J // CH)]
+        y_bf = [tile([P, CH * PACK], BF16, "y_bf%d" % c) for c in range(J // CH)]
+        y_w = [tile([P, CH], U32, "y_w%d" % c) for c in range(J // CH)]
+        y_s = tile([P, J], U8, "y_s")
+        out_rows = out_0.rearrange("(p t) j -> p t j", t=PACK)
+        out_words = out_1[0].rearrange("p c r -> p (c r)").bitcast(I32)
+
+        def subtract(c):
+            nc.vector.tensor_tensor(out=diff[c][:], in0=p_banks[c][:].rearrange("p t j -> p j t"), in1=q_off[c][:], op=ALU.add)
+            nc.scalar.activation(
+                out=y[c][:].rearrange("p t (b i) -> p b t i", i=4),
+                in_=diff[c][:].rearrange("p (b i) t -> p b t i", i=4),
+                func=ACT.Relu,
+            )
+            nc.sync.dma_start(out=out_rows[:, :, c * CH : (c + 1) * CH], in_=y[c][:])
+
+        def round_y(c):
+            nc.vector.tensor_scalar(
+                out=y_bf[c][:], in0=diff[c][:].rearrange("p j t -> p (j t)"), scalar1=0.0, scalar2=None, op0=ALU.max
+            )
+
+        def quantise_y(c):
+            nc.vector.quantize_mx(out=y_w[c][:].bitcast(FP8X4), scales=y_s[:, c * CH : (c + 1) * CH], in_=y_bf[c][:])
+            nc.sync.dma_start(out=out_words[:, c * CH : (c + 1) * CH], in_=y_w[c][:].bitcast(I32))
+
+        subtract(0)
+        subtract(1)
+        round_y(0)
+        subtract(2)
+        round_y(1)
+        quantise_y(0)
+        subtract(3)
+        round_y(2)
+        quantise_y(1)
+        round_y(3)
+        quantise_y(2)
+        quantise_y(3)
+        for q in range(4):
+            engine = nc.sync if q % 2 == 0 else nc.scalar
+            engine.dma_start(out=out_2[0, 4 * q : 4 * q + 4, :].bitcast(I32), in_=y_s[32 * q : 32 * q + 4, :].bitcast(I32))

@@ -31,8 +31,8 @@ def tile_moe_expert_heads_against_shared_pl_kernel(
         sb = ctx.enter_context(tc.tile_pool(name="sb", bufs=1))
         ps = ctx.enter_context(tc.psum_pool(name="ps", bufs=1))
 
-        def tile(shape, dtype, name):
-            return sb.tile(shape, dtype, name=name, align_bytes=64)
+        def tile(shape, dtype, name, tag=None):
+            return sb.tile(shape, dtype, name=name, tag=tag or name, align_bytes=64)
 
         lists = sb.tile([P, J // 16], U16, name="lists")
         list2 = sb.tile([P, J // 16], U16, name="list2")
@@ -53,22 +53,21 @@ def tile_moe_expert_heads_against_shared_pl_kernel(
             rows = xt.rearrange("(p t) c -> p t c", t=PACK)
             nc.sync.dma_start(out=raw[u][h][:], in_=rows[:, 2 * u : 2 * u + 2, h * HALF : (h + 1) * HALF])
 
-        nc.vector.memset(xb_s[:].bitcast(I32), 0)
-        nc.vector.memset(wb_s[:].bitcast(I32), 0)
-        nc.gpsimd.memset(wa_s[:].bitcast(I32), 0)
+        for plane in (xb_s, wb_s, wa_s):
+            nc.vector.memset(plane[:].bitcast(I32), 0)
 
         nc.sync.dma_start(list2[:], offs2)
         nc.sync.dma_start(lists[:], offs)
         nc.sync.dma_start(out=xb_w[:].bitcast(I32), in_=xb_words[0].rearrange("p c r -> p (c r)").bitcast(I32))
-        load_xt(0, 0)
         load_scales(nc.sync, xb_s, xb_scales, range(4))
-        load_scales(nc.gpsimd, wa_s, wa_scales, range(4))
+        load_xt(0, 0)
         load_xt(0, 1)
         nc.sync.dma_start(out=wb_w[:].bitcast(I32), in_=wb_words[0].bitcast(I32))
-        load_xt(1, 0)
         load_scales(nc.sync, wb_s, wb_scales, range(4))
+        load_xt(1, 0)
         load_xt(1, 1)
         nc.sync.dma_start(out=wa_w[:].bitcast(I32), in_=wa_words[0].bitcast(I32))
+        load_scales(nc.sync, wa_s, wa_scales, range(4))
 
         def cast(engine, u, h, lo, hi):
             dst = pairs[u][:].bitcast(BF16).rearrange("p (c e) -> p c e", e=2)[:, h * HALF + lo : h * HALF + hi, :]
@@ -110,37 +109,41 @@ def tile_moe_expert_heads_against_shared_pl_kernel(
         nc.vector.tensor_copy(out=xbg_s[:], in_=xb_s[:].indirect(list2[:]))
         cast("scalar", 0, 1, 0, HALF)
 
-        picked = [tile([P, 2, GCH], F32, "picked%d" % g) for g in range(J // GCH)]
-
-        def gather(u, g):
-            cols = GCH // 16
-            nc.vector.tensor_copy(out=picked[g][:, u, :], in_=pairs[u][:].indirect(lists[:, g * cols : (g + 1) * cols]))
-
-        gather(0, 0)
-        gather(0, 1)
-        cast("scalar", 1, 0, 0, HALF)
         wb = deal(wb_w, wb_s, "wbd")
         q_banks = [ps.tile([P, PACK, CH], F32, name="q%d" % c) for c in range(J // CH)]
         for c in range(J // CH):
             product(q_banks[c], wb, xbg_w, xbg_s, c * CH)
+
+        picked = tile([P, 2, J], F32, "picked", tag="wb_s")
+
+        def gather(u):
+            nc.vector.tensor_copy(out=picked[:, u, :], in_=pairs[u][:].indirect(lists[:]))
+
+        gather(0)
+        cast("scalar", 1, 0, 0, HALF)
         SPLIT = 176
         cast("scalar", 1, 1, 0, SPLIT)
         cast("vector", 1, 1, SPLIT, HALF)
 
-        q_off = [tile([P, CH, PACK], F32, "q_off%d" % c) for c in range(J // CH)]
-        for c in range(J // CH):
-            nc.scalar.activation(out=q_off[c][:], in_=q_banks[c][:].rearrange("p t j -> p j t"), func=ACT.Copy, scale=-0.7)
+        q_off = tile([P, J // CH, CH * PACK], F32, "q_off", tag="raw11")
+
+        def take_off(c):
+            nc.scalar.activation(
+                out=q_off[:, c, :].rearrange("p (j t) -> p j t", t=PACK),
+                in_=q_banks[c][:].rearrange("p t j -> p j t"),
+                func=ACT.Copy,
+                scale=-0.7,
+            )
 
         woven = [tile([P, GCH, 2], F32, "woven%d" % g) for g in range(J // GCH)]
         x_w = [tile([P, GCH], U32, "x_w%d" % g) for g in range(J // GCH)]
-        x_s = [tile([P, GCH], U8, "x_s%d" % g) for g in range(J // GCH)]
 
         def weave(g):
-            nc.vector.tensor_copy(out=woven[g][:], in_=picked[g][:].rearrange("p u j -> p j u"))
+            nc.scalar.copy(out=woven[g][:], in_=picked[:, :, g * GCH : (g + 1) * GCH].rearrange("p u j -> p j u"))
 
         def quantise_x(g):
             nc.vector.quantize_mx(
-                out=x_w[g][:].bitcast(FP8X4), scales=x_s[g][:], in_=woven[g][:].rearrange("p j u -> p (j u)").bitcast(BF16)
+                out=x_w[g][:].bitcast(FP8X4), scales=x_s[g], in_=woven[g][:].rearrange("p j u -> p (j u)").bitcast(BF16)
             )
 
         p_banks = [ps.tile([P, PACK, CH], F32, name="p%d" % c) for c in range(J // CH)]
@@ -149,13 +152,18 @@ def tile_moe_expert_heads_against_shared_pl_kernel(
             for c in range(g * GCH // CH, (g + 1) * GCH // CH):
                 product(p_banks[c], wa, x_w[g], x_s[g], c * CH - g * GCH)
 
-        gather(1, 0)
+        gather(1)
+        take_off(0)
+        take_off(1)
         weave(0)
+        weave(1)
+        take_off(2)
+        take_off(3)
         wa = deal(wa_w, wa_s, "wad")
+        x_plane = tile([P, J], U8, "x_plane", tag="wa_s")
+        x_s = [x_plane[:, g * GCH : (g + 1) * GCH] for g in range(J // GCH)]
         quantise_x(0)
         routed(0)
-        gather(1, 1)
-        weave(1)
         quantise_x(1)
         routed(1)
 
@@ -168,7 +176,14 @@ def tile_moe_expert_heads_against_shared_pl_kernel(
         out_words = out_1[0].rearrange("p c r -> p (c r)").bitcast(I32)
 
         def subtract(c):
-            nc.vector.tensor_tensor(out=diff[c][:], in0=p_banks[c][:].rearrange("p t j -> p j t"), in1=q_off[c][:], op=ALU.add)
+            nc.vector.tensor_tensor(
+                out=diff[c][:],
+                in0=p_banks[c][:].rearrange("p t j -> p j t"),
+                in1=q_off[:, c, :].rearrange("p (j t) -> p j t", t=PACK),
+                op=ALU.add,
+            )
+
+        def relu_store(c):
             nc.scalar.activation(
                 out=y[c][:].rearrange("p t (b i) -> p b t i", i=4),
                 in_=diff[c][:].rearrange("p (b i) t -> p b t i", i=4),
@@ -176,25 +191,31 @@ def tile_moe_expert_heads_against_shared_pl_kernel(
             )
             nc.sync.dma_start(out=out_rows[:, :, c * CH : (c + 1) * CH], in_=y[c][:])
 
-        def round_y(c):
-            nc.vector.tensor_scalar(
-                out=y_bf[c][:], in0=diff[c][:].rearrange("p j t -> p (j t)"), scalar1=0.0, scalar2=None, op0=ALU.max
-            )
+        def round_y(c, engine):
+            flat = diff[c][:].rearrange("p j t -> p (j t)")
+            if engine == "scalar":
+                nc.scalar.activation(out=y_bf[c][:], in_=flat, func=ACT.Relu)
+            else:
+                nc.vector.tensor_scalar(out=y_bf[c][:], in0=flat, scalar1=0.0, scalar2=None, op0=ALU.max)
 
         def quantise_y(c):
             nc.vector.quantize_mx(out=y_w[c][:].bitcast(FP8X4), scales=y_s[:, c * CH : (c + 1) * CH], in_=y_bf[c][:])
             nc.sync.dma_start(out=out_words[:, c * CH : (c + 1) * CH], in_=y_w[c][:].bitcast(I32))
 
         subtract(0)
+        relu_store(0)
+        round_y(0, "scalar")
         subtract(1)
-        round_y(0)
+        relu_store(1)
         subtract(2)
-        round_y(1)
-        quantise_y(0)
+        relu_store(2)
+        round_y(1, "vector")
         subtract(3)
-        round_y(2)
+        relu_store(3)
+        quantise_y(0)
+        round_y(2, "vector")
         quantise_y(1)
-        round_y(3)
+        round_y(3, "vector")
         quantise_y(2)
         quantise_y(3)
         for q in range(4):

@@ -42,7 +42,8 @@ def tile_moe_expert_heads_against_shared_pl_kernel(
         wb_w = tile([P, 2 * N], U8, "wb_w")
         wa_s = tile([P, N], U8, "wa_s")
         wb_s = tile([P, N], U8, "wb_s")
-        raw = [[tile([P, 2, HALF], F32, "raw%d%d" % (u, h)) for h in range(2)] for u in range(2)]
+        cuts = [[0, T // 2, T], [0, T // 2, T]]
+        raw = [[tile([P, 2, cuts[u][h + 1] - cuts[u][h]], F32, "raw%d%d" % (u, h)) for h in range(2)] for u in range(2)]
         pairs = [tile([P, T], F32, "pairs%d" % u) for u in range(2)]
 
         def load_scales(engine, plane, rows, quads):
@@ -51,14 +52,14 @@ def tile_moe_expert_heads_against_shared_pl_kernel(
 
         def load_xt(u, h):
             rows = xt.rearrange("(p t) c -> p t c", t=PACK)
-            nc.sync.dma_start(out=raw[u][h][:], in_=rows[:, 2 * u : 2 * u + 2, h * HALF : (h + 1) * HALF])
+            nc.sync.dma_start(out=raw[u][h][:], in_=rows[:, 2 * u : 2 * u + 2, cuts[u][h] : cuts[u][h + 1]])
 
         for plane in (xb_s, wb_s, wa_s):
             nc.vector.memset(plane[:].bitcast(I32), 0)
 
         nc.sync.dma_start(list2[:], offs2)
-        nc.sync.dma_start(lists[:], offs)
         nc.sync.dma_start(out=xb_w[:].bitcast(I32), in_=xb_words[0].rearrange("p c r -> p (c r)").bitcast(I32))
+        nc.sync.dma_start(lists[:], offs)
         load_scales(nc.sync, xb_s, xb_scales, range(4))
         load_xt(0, 0)
         load_xt(0, 1)
@@ -90,134 +91,113 @@ def tile_moe_expert_heads_against_shared_pl_kernel(
             )
             return dealt_w, dealt_s
 
-        def product(bank, w, codes, scales, lo):
-            for t in range(PACK):
+        def product(bank, w, codes, scales, v):
+            for e in range(2):
+                t = 2 * v + e
                 nc.tensor.matmul_mx(
-                    out=bank[:, t, :],
+                    out=bank[:, e, :],
                     lhsT=w[0][:, 2 * P * t : 2 * P * (t + 1)].bitcast(FP4X4),
                     lhsT_scale=w[1][:, P * t : P * (t + 1)],
-                    rhs=codes[:, lo : lo + CH].bitcast(FP8X4),
-                    rhs_scale=scales[:, lo : lo + CH],
+                    rhs=codes.bitcast(FP8X4),
+                    rhs_scale=scales,
                     start=True,
                     stop=True,
                 )
+
+        parts = [(g, v) for g in range(2) for v in range(2)]
 
         xbg_w = tile([P, J], U32, "xbg_w")
         xbg_s = tile([P, J], U8, "xbg_s")
         nc.vector.tensor_copy(out=xbg_w[:], in_=xb_w[:].indirect(list2[:]))
         cast("scalar", 0, 0, 0, HALF)
         nc.vector.tensor_copy(out=xbg_s[:], in_=xb_s[:].indirect(list2[:]))
-        cast("scalar", 0, 1, 0, HALF)
+        cast("scalar", 0, 1, 0, 320)
+        cast("vector", 0, 1, 320, HALF)
 
         wb = deal(wb_w, wb_s, "wbd")
-        q_banks = [ps.tile([P, PACK, CH], F32, name="q%d" % c) for c in range(J // CH)]
-        for c in range(J // CH):
-            product(q_banks[c], wb, xbg_w, xbg_s, c * CH)
+        q_banks = {part: ps.tile([P, 2, GCH], F32, name="q%d%d" % part) for part in parts}
+        for g, v in parts:
+            product(q_banks[g, v], wb, xbg_w[:, g * GCH : (g + 1) * GCH], xbg_s[:, g * GCH : (g + 1) * GCH], v)
 
         picked = tile([P, 2, J], F32, "picked", tag="wb_s")
 
-        def gather(u):
-            nc.vector.tensor_copy(out=picked[:, u, :], in_=pairs[u][:].indirect(lists[:]))
+        def gather(u, lo, hi):
+            nc.vector.tensor_copy(out=picked[:, u, lo:hi], in_=pairs[u][:].indirect(lists[:, lo // 16 : hi // 16]))
 
-        gather(0)
+        gather(0, 0, J)
         cast("scalar", 1, 0, 0, HALF)
         SPLIT = 176
         cast("scalar", 1, 1, 0, SPLIT)
         cast("vector", 1, 1, SPLIT, HALF)
 
-        q_off = tile([P, J // CH, CH * PACK], F32, "q_off", tag="raw11")
+        q_off = []
 
-        def take_off(c):
-            nc.scalar.activation(
-                out=q_off[:, c, :].rearrange("p (j t) -> p j t", t=PACK),
-                in_=q_banks[c][:].rearrange("p t j -> p j t"),
-                func=ACT.Copy,
-                scale=-0.7,
-            )
+        def take_off(g, v):
+            nc.scalar.activation(out=q_off[g][:, 2 * v : 2 * v + 2, :], in_=q_banks[g, v][:], func=ACT.Copy, scale=-0.7)
 
-        woven = [tile([P, GCH, 2], F32, "woven%d" % g) for g in range(J // GCH)]
-        x_w = [tile([P, GCH], U32, "x_w%d" % g) for g in range(J // GCH)]
+        woven = [tile([P, GCH, 2], F32, "woven%d" % g) for g in range(2)]
+        x_w = [tile([P, GCH], U32, "x_w%d" % g) for g in range(2)]
 
         def weave(g):
             nc.scalar.copy(out=woven[g][:], in_=picked[:, :, g * GCH : (g + 1) * GCH].rearrange("p u j -> p j u"))
 
-        def quantise_x(g):
-            nc.vector.quantize_mx(
-                out=x_w[g][:].bitcast(FP8X4), scales=x_s[g], in_=woven[g][:].rearrange("p j u -> p (j u)").bitcast(BF16)
-            )
-
-        p_banks = [ps.tile([P, PACK, CH], F32, name="p%d" % c) for c in range(J // CH)]
-
-        def routed(g):
-            for c in range(g * GCH // CH, (g + 1) * GCH // CH):
-                product(p_banks[c], wa, x_w[g], x_s[g], c * CH - g * GCH)
-
-        gather(1)
-        take_off(0)
-        take_off(1)
+        gather(1, 0, GCH)
+        gather(1, GCH, J)
+        q_off.append(tile([P, PACK, GCH], F32, "q_off0", tag="raw11"))
+        take_off(0, 0)
+        take_off(0, 1)
         weave(0)
         weave(1)
-        take_off(2)
-        take_off(3)
+        q_off.append(tile([P, PACK, GCH], F32, "q_off1", tag="wb_s"))
+        take_off(1, 0)
+        take_off(1, 1)
+
         wa = deal(wa_w, wa_s, "wad")
         x_plane = tile([P, J], U8, "x_plane", tag="wa_s")
-        x_s = [x_plane[:, g * GCH : (g + 1) * GCH] for g in range(J // GCH)]
-        quantise_x(0)
-        routed(0)
-        quantise_x(1)
-        routed(1)
+        p_banks = {part: ps.tile([P, 2, GCH], F32, name="p%d%d" % part) for part in parts}
+        for g in range(2):
+            x_s = x_plane[:, g * GCH : (g + 1) * GCH]
+            nc.vector.quantize_mx(
+                out=x_w[g][:].bitcast(FP8X4), scales=x_s, in_=woven[g][:].rearrange("p j u -> p (j u)").bitcast(BF16)
+            )
+            for v in range(2):
+                product(p_banks[g, v], wa, x_w[g][:], x_s, v)
 
-        diff = [tile([P, CH, PACK], F32, "diff%d" % c) for c in range(J // CH)]
-        y = [tile([P, PACK, CH], F32, "y%d" % c) for c in range(J // CH)]
-        y_bf = [tile([P, CH * PACK], BF16, "y_bf%d" % c) for c in range(J // CH)]
-        y_w = [tile([P, CH], U32, "y_w%d" % c) for c in range(J // CH)]
+        diff = [tile([P, PACK, GCH], F32, "diff%d" % g) for g in range(2)]
+        y = {part: tile([P, 2, GCH], F32, "y%d%d" % part) for part in parts}
+        y_bf = tile([P, J * PACK], BF16, "y_bf")
+        y_w = tile([P, J], U32, "y_w")
         y_s = tile([P, J], U8, "y_s")
         out_rows = out_0.rearrange("(p t) j -> p t j", t=PACK)
         out_words = out_1[0].rearrange("p c r -> p (c r)").bitcast(I32)
 
-        def subtract(c):
-            nc.vector.tensor_tensor(
-                out=diff[c][:],
-                in0=p_banks[c][:].rearrange("p t j -> p j t"),
-                in1=q_off[:, c, :].rearrange("p (j t) -> p j t", t=PACK),
-                op=ALU.add,
-            )
+        for g, v in parts:
+            rows = slice(2 * v, 2 * v + 2)
+            nc.vector.tensor_tensor(out=diff[g][:, rows, :], in0=p_banks[g, v][:], in1=q_off[g][:, rows, :], op=ALU.add)
+            nc.scalar.activation(out=y[g, v][:], in_=diff[g][:, rows, :], func=ACT.Relu)
+            nc.sync.dma_start(out=out_rows[:, rows, g * GCH : (g + 1) * GCH], in_=y[g, v][:])
 
-        def relu_store(c):
-            nc.scalar.activation(
-                out=y[c][:].rearrange("p t (b i) -> p b t i", i=4),
-                in_=diff[c][:].rearrange("p (b i) t -> p b t i", i=4),
-                func=ACT.Relu,
-            )
-            nc.sync.dma_start(out=out_rows[:, :, c * CH : (c + 1) * CH], in_=y[c][:])
-
-        def round_y(c, engine):
-            flat = diff[c][:].rearrange("p j t -> p (j t)")
+        def round_y(engine, g, lo, hi):
+            src = diff[g][:, :, lo:hi].rearrange("p t (c i) -> p c t i", i=4)
+            dst = y_bf[:, (g * GCH + lo) * PACK : (g * GCH + hi) * PACK].rearrange("p (c i t) -> p c t i", i=4, t=PACK)
             if engine == "scalar":
-                nc.scalar.activation(out=y_bf[c][:], in_=flat, func=ACT.Relu)
+                nc.scalar.activation(out=dst, in_=src, func=ACT.Relu)
             else:
-                nc.vector.tensor_scalar(out=y_bf[c][:], in0=flat, scalar1=0.0, scalar2=None, op0=ALU.max)
+                nc.vector.tensor_scalar(out=dst, in0=src, scalar1=0.0, scalar2=None, op0=ALU.max)
 
-        def quantise_y(c):
-            nc.vector.quantize_mx(out=y_w[c][:].bitcast(FP8X4), scales=y_s[:, c * CH : (c + 1) * CH], in_=y_bf[c][:])
-            nc.sync.dma_start(out=out_words[:, c * CH : (c + 1) * CH], in_=y_w[c][:].bitcast(I32))
+        def quantise_y(g):
+            cols = slice(g * GCH, (g + 1) * GCH)
+            nc.vector.quantize_mx(
+                out=y_w[:, cols].bitcast(FP8X4), scales=y_s[:, cols], in_=y_bf[:, g * GCH * PACK : (g + 1) * GCH * PACK]
+            )
+            nc.sync.dma_start(out=out_words[:, cols], in_=y_w[:, cols].bitcast(I32))
 
-        subtract(0)
-        relu_store(0)
-        round_y(0, "scalar")
-        subtract(1)
-        relu_store(1)
-        subtract(2)
-        relu_store(2)
-        round_y(1, "vector")
-        subtract(3)
-        relu_store(3)
+        TAIL = 160
+        round_y("vector", 0, 0, GCH)
+        round_y("vector", 1, 0, TAIL)
+        round_y("scalar", 1, TAIL, GCH)
         quantise_y(0)
-        round_y(2, "vector")
         quantise_y(1)
-        round_y(3, "vector")
-        quantise_y(2)
-        quantise_y(3)
         for q in range(4):
             engine = nc.sync if q % 2 == 0 else nc.scalar
             engine.dma_start(out=out_2[0, 4 * q : 4 * q + 4, :].bitcast(I32), in_=y_s[32 * q : 32 * q + 4, :].bitcast(I32))

from contextlib import ExitStack

import concourse.mybir as mybir

K, T, J, L, S, N = 512, 1024, 512, 512, 1024, 512
FLOPS = 2 * K * N * J + 2 * L * N * J

F32 = mybir.dt.float32
BF16 = mybir.dt.bfloat16
I32 = mybir.dt.int32
U32 = mybir.dt.uint32
U16 = mybir.dt.uint16
U8 = mybir.dt.uint8
FP8X4 = mybir.dt.float8_e4m3fn_x4
FP4X4 = mybir.dt.float4_e2m1fn_x4
ACT = mybir.ActivationFunctionType
ALU = mybir.AluOpType

P = 128
PACK = 4
CH = 128
GCH = 256
HALF = T // 2


def tile_moe_expert_heads_against_shared_pl_kernel(
    tc, xt, wa_words, wa_scales, xb_words, xb_scales, wb_words, wb_scales, offs, offs2, out_0, out_1, out_2
):
    nc = tc.nc
    with ExitStack() as ctx:
        sb = ctx.enter_context(tc.tile_pool(name="sb", bufs=1))
        ps = ctx.enter_context(tc.psum_pool(name="ps", bufs=1))

        def tile(shape, dtype, name, tag=None):
            return sb.tile(shape, dtype, name=name, tag=tag or name, align_bytes=64)

        lists = sb.tile([P, J // 16], U16, name="lists")
        list2 = sb.tile([P, J // 16], U16, name="list2")
        xb_w = tile([P, S], U32, "xb_w")
        xb_s = tile([P, S], U8, "xb_s")
        wa_w = tile([P, 2 * N], U8, "wa_w")
        wb_w = tile([P, 2 * N], U8, "wb_w")
        wa_s = tile([P, N], U8, "wa_s")
        wb_s = tile([P, N], U8, "wb_s")
        cuts = [[0, T // 2, T], [0, T // 2, T]]
        raw = [[tile([P, 2, cuts[u][h + 1] - cuts[u][h]], F32, "raw%d%d" % (u, h)) for h in range(2)] for u in range(2)]
        pairs = [tile([P, T], F32, "pairs%d" % u) for u in range(2)]

        def load_scales(engine, plane, rows, quads):
            for q in quads:
                engine.dma_start(out=plane[32 * q : 32 * q + 4, :].bitcast(I32), in_=rows[0, 4 * q : 4 * q + 4, :].bitcast(I32))

        def load_xt(u, h):
            rows = xt.rearrange("(p t) c -> p t c", t=PACK)
            nc.sync.dma_start(out=raw[u][h][:], in_=rows[:, 2 * u : 2 * u + 2, cuts[u][h] : cuts[u][h + 1]])

        for plane in (xb_s, wb_s, wa_s):
            nc.vector.memset(plane[:].bitcast(I32), 0)

        nc.sync.dma_start(list2[:], offs2)
        nc.sync.dma_start(out=xb_w[:].bitcast(I32), in_=xb_words[0].rearrange("p c r -> p (c r)").bitcast(I32))
        nc.sync.dma_start(lists[:], offs)
        load_scales(nc.sync, xb_s, xb_scales, range(4))
        load_xt(0, 0)
        load_xt(0, 1)
        nc.sync.dma_start(out=wb_w[:].bitcast(I32), in_=wb_words[0].bitcast(I32))
        load_scales(nc.sync, wb_s, wb_scales, range(4))
        load_xt(1, 0)
        load_xt(1, 1)
        nc.sync.dma_start(out=wa_w[:].bitcast(I32), in_=wa_words[0].bitcast(I32))
        load_scales(nc.sync, wa_s, wa_scales, range(4))

        def cast(engine, u, h, lo, hi):
            dst = pairs[u][:].bitcast(BF16).rearrange("p (c e) -> p c e", e=2)[:, h * HALF + lo : h * HALF + hi, :]
            src = raw[u][h][:, :, lo:hi].rearrange("p e c -> p c e")
            if engine == "scalar":
                nc.scalar.activation(out=dst, in_=src, func=ACT.Copy)
            else:
                nc.vector.tensor_copy(out=dst, in_=src)

        def deal(words, plane, name):
            dealt_w = tile([P, 2 * N], U8, name + "_w")
            dealt_s = tile([P, N], U8, name + "_s")
            nc.vector.tensor_copy(
                out=dealt_w[:].bitcast(U16).rearrange("p (t b i) -> p b t i", t=PACK, i=8),
                in_=words[:].bitcast(U16).rearrange("p (b i t) -> p b t i", t=PACK, i=8),
            )
            nc.vector.tensor_copy(
                out=dealt_s[:].rearrange("p (t b i) -> p b t i", t=PACK, i=16),
                in_=plane[:].rearrange("p (b i t) -> p b t i", t=PACK, i=16),
            )
            return dealt_w, dealt_s

        def product(bank, w, codes, scales, v):
            for e in range(2):
                t = 2 * v + e
                nc.tensor.matmul_mx(
                    out=bank[:, e, :],
                    lhsT=w[0][:, 2 * P * t : 2 * P * (t + 1)].bitcast(FP4X4),
                    lhsT_scale=w[1][:, P * t : P * (t + 1)],
                    rhs=codes.bitcast(FP8X4),
                    rhs_scale=scales,
                    start=True,
                    stop=True,
                )

        parts = [(g, v) for g in range(2) for v in range(2)]

        xbg_w = tile([P, J], U32, "xbg_w")
        xbg_s = tile([P, J], U8, "xbg_s")
        nc.vector.tensor_copy(out=xbg_w[:], in_=xb_w[:].indirect(list2[:]))
        cast("scalar", 0, 0, 0, HALF)
        nc.vector.tensor_copy(out=xbg_s[:], in_=xb_s[:].indirect(list2[:]))
        cast("scalar", 0, 1, 0, 320)
        cast("vector", 0, 1, 320, HALF)

        wb = deal(wb_w, wb_s, "wbd")
        q_banks = {part: ps.tile([P, 2, GCH], F32, name="q%d%d" % part) for part in parts}
        for g, v in parts:
            product(q_banks[g, v], wb, xbg_w[:, g * GCH : (g + 1) * GCH], xbg_s[:, g * GCH : (g + 1) * GCH], v)

        picked = tile([P, 2, J], F32, "picked", tag="wb_s")

        def gather(u, lo, hi):
            nc.vector.tensor_copy(out=picked[:, u, lo:hi], in_=pairs[u][:].indirect(lists[:, lo // 16 : hi // 16]))

        gather(0, 0, J)
        cast("scalar", 1, 0, 0, HALF)
        SPLIT = 176
        cast("scalar", 1, 1, 0, SPLIT)
        cast("vector", 1, 1, SPLIT, HALF)

        q_off = []

        def take_off(g, v):
            nc.scalar.activation(out=q_off[g][:, 2 * v : 2 * v + 2, :], in_=q_banks[g, v][:], func=ACT.Copy, scale=-0.7)

        woven = [tile([P, GCH, 2], F32, "woven%d" % g) for g in range(2)]
        x_w = [tile([P, GCH], U32, "x_w%d" % g) for g in range(2)]

        def weave(g):
            nc.scalar.copy(out=woven[g][:], in_=picked[:, :, g * GCH : (g + 1) * GCH].rearrange("p u j -> p j u"))

        gather(1, 0, GCH)
        gather(1, GCH, J)
        q_off.append(tile([P, PACK, GCH], F32, "q_off0", tag="raw11"))
        take_off(0, 0)
        take_off(0, 1)
        weave(0)
        weave(1)
        q_off.append(tile([P, PACK, GCH], F32, "q_off1", tag="wb_s"))
        take_off(1, 0)
        take_off(1, 1)

        wa = deal(wa_w, wa_s, "wad")
        x_plane = tile([P, J], U8, "x_plane", tag="wa_s")
        p_banks = {part: ps.tile([P, 2, GCH], F32, name="p%d%d" % part) for part in parts}
        for g in range(2):
            x_s = x_plane[:, g * GCH : (g + 1) * GCH]
            nc.vector.quantize_mx(
                out=x_w[g][:].bitcast(FP8X4), scales=x_s, in_=woven[g][:].rearrange("p j u -> p (j u)").bitcast(BF16)
            )
            for v in range(2):
                product(p_banks[g, v], wa, x_w[g][:], x_s, v)

        diff = [tile([P, PACK, GCH], F32, "diff%d" % g) for g in range(2)]
        y = {part: tile([P, 2, GCH], F32, "y%d%d" % part) for part in parts}
        y_bf = tile([P, J * PACK], BF16, "y_bf")
        y_w = tile([P, J], U32, "y_w")
        y_s = tile([P, J], U8, "y_s")
        out_rows = out_0.rearrange("(p t) j -> p t j", t=PACK)
        out_words = out_1[0].rearrange("p c r -> p (c r)").bitcast(I32)

        for g, v in parts:
            rows = slice(2 * v, 2 * v + 2)
            nc.vector.tensor_tensor(out=diff[g][:, rows, :], in0=p_banks[g, v][:], in1=q_off[g][:, rows, :], op=ALU.add)
            nc.scalar.activation(out=y[g, v][:], in_=diff[g][:, rows, :], func=ACT.Relu)
            nc.sync.dma_start(out=out_rows[:, rows, g * GCH : (g + 1) * GCH], in_=y[g, v][:])

        def round_y(engine, g, lo, hi):
            src = diff[g][:, :, lo:hi].rearrange("p t (c i) -> p c t i", i=4)
            dst = y_bf[:, (g * GCH + lo) * PACK : (g * GCH + hi) * PACK].rearrange("p (c i t) -> p c t i", i=4, t=PACK)
            if engine == "scalar":
                nc.scalar.activation(out=dst, in_=src, func=ACT.Relu)
            else:
                nc.vector.tensor_scalar(out=dst, in0=src, scalar1=0.0, scalar2=None, op0=ALU.max)

        def quantise_y(g):
            cols = slice(g * GCH, (g + 1) * GCH)
            nc.vector.quantize_mx(
                out=y_w[:, cols].bitcast(FP8X4), scales=y_s[:, cols], in_=y_bf[:, g * GCH * PACK : (g + 1) * GCH * PACK]
            )
            nc.sync.dma_start(out=out_words[:, cols], in_=y_w[:, cols].bitcast(I32))

        TAIL = 160
        round_y("vector", 0, 0, GCH)
        round_y("vector", 1, 0, TAIL)
        round_y("scalar", 1, TAIL, GCH)
        quantise_y(0)
        quantise_y(1)
        for q in range(4):
            engine = nc.sync if q % 2 == 0 else nc.scalar
            engine.dma_start(out=out_2[0, 4 * q : 4 * q + 4, :].bitcast(I32), in_=y_s[32 * q : 32 * q + 4, :].bitcast(I32))
